import numpy as np
CORES = [24,25,26,27,28,29,30,31,152,153,154,155,156,157,158,159]
N = 16
COUNTS = [[0,0,16,16,0,16,8,8,0,64,8,16,8,8,16,0],[16,0,16,8,16,0,0,8,0,64,16,8,8,16,0,8],[8,8,0,16,16,16,8,8,16,64,0,8,16,16,16,16],[8,16,8,0,0,16,16,8,16,64,8,0,0,16,8,8],[8,16,8,16,0,16,8,16,8,64,8,16,0,16,16,0],[16,8,8,0,8,0,0,8,16,64,16,0,0,16,8,0],[16,16,0,8,16,8,0,16,0,64,16,8,8,0,0,0],[8,8,8,8,8,16,16,0,8,64,8,16,8,16,16,16],[0,8,16,16,16,16,8,16,0,64,8,16,16,16,8,16],[8,8,0,8,8,16,16,8,0,0,16,8,16,0,8,0],[8,16,16,16,8,16,8,8,8,64,0,16,16,0,0,16],[8,16,16,8,0,8,0,8,16,64,8,0,16,0,8,8],[16,8,8,16,8,0,8,16,0,64,8,0,0,8,16,16],[16,8,8,16,16,8,8,8,8,64,16,16,0,0,16,16],[8,16,0,0,0,8,8,16,16,64,0,8,16,16,0,8],[16,0,16,0,16,16,16,8,8,64,8,16,16,16,16,0]]
XW, YW = 240, 960
def setup_inputs(rng):
    return {"x": rng.standard_normal((N, 128, XW), dtype=np.float32)}
def reference(x):
    y = np.full((N, 128, YW), np.nan, x.dtype)
    fill = [0] * N
    for s in range(N):
        o = 0
        for d in range(N):
            c = COUNTS[s][d]
            y[d][:, fill[d]:fill[d] + c] = x[s][:, o:o + c]
            o += c; fill[d] += c
    return {"y": y}

@@ -1,0 +1,43 @@
+SCRATCH = {
+    "xs": ("sbuf", [128, 240], "float32"),
+    "land": ("sbuf", [128, 960], "float32"),
+}
+SEMAPHORES = ["loaded", "arrived", "stored"]
+
+
+def _engines(mask):
+    return bin(mask).count("1")
+
+
+def rank_program(g, core, T, topo):
+    me = T.rank_of(core)
+    if me is None:
+        return
+    counts = T.tables["COUNTS"]
+    n = len(counts)
+    cores = T.cores
+
+    held = sum(counts[me])
+    owed = sum(counts[s][me] for s in range(n))
+
+    g.dma_start(T.xs[:, 0:held], T.x[:, 0:held]).then_inc(T.sem.loaded, 16)
+    g.wait_ge(T.sem.loaded, 16)
+
+    order = sorted((d for d in range(n) if counts[me][d] > 0),
+                   key=lambda d: (topo.host(cores[d]) == topo.host(core), -counts[me][d], d))
+    expect = 0
+    for d in order:
+        c = counts[me][d]
+        src = sum(counts[me][:d])
+        dst = sum(counts[s][d] for s in range(me))
+        rid, pid = topo.addr(cores[d], core)
+        mask = topo.mask(core, cores[d])
+        g.remote_dma(T.land[:, dst:dst + c], T.xs[:, src:src + c], T.sem.arrived, T.sem.arrived, pid, rid, mask)
+        expect += _engines(mask)
+
+    for s in range(n):
+        if counts[s][me] > 0:
+            expect += _engines(topo.mask(cores[s], core))
+    g.wait_ge(T.sem.arrived, expect)
+    g.dma_start(T.y[:, 0:owed], T.land[:, 0:owed]).then_inc(T.sem.stored, 16)
+    g.wait_ge(T.sem.stored, 16)

@@ -1,8 +1,39 @@
+from concourse.bass import DstId, RemoteDMATransfer
+
 SCRATCH = {
     "xs": ("sbuf", [128, 240], "float32"),
     "land": ("sbuf", [128, 960], "float32"),
 }
-SEMAPHORES = ["loaded", "arrived", "stored"]
+SEMAPHORES = ["loaded", "far", "near", "sent", "stored"]
+
+
+def _pow2_groups(items):
+    out, i = [], 0
+    while i < len(items):
+        k = 8
+        while k > len(items) - i:
+            k //= 2
+        out.append(items[i:i + k])
+        i += k
+    return out
+
+
+def _plan(s, counts, cores, topo):
+    n = len(counts)
+    calls = []
+    for w in sorted({c for c in counts[s] if c > 0}, reverse=True):
+        dests = [d for d in range(n) if counts[s][d] == w]
+        far = _pow2_groups([d for d in dests if topo.same_plane(cores[s], cores[d])])
+        near = _pow2_groups([d for d in dests if not topo.same_plane(cores[s], cores[d])])
+        for i in range(max(len(far), len(near))):
+            call = []
+            for base, groups, is_far in ((0, far, True), (8, near, False)):
+                if i < len(groups):
+                    e = 8 // len(groups[i])
+                    for j, d in enumerate(groups[i]):
+                        call.append((d, ((1 << e) - 1) << (base + j * e), is_far))
+            calls.append(call)
+    return calls
 
 
 def _engines(mask):
@@ -18,26 +49,43 @@ def rank_program(g, core, T, topo):
     cores = T.cores
 
     held = sum(counts[me])
-    owed = sum(counts[s][me] for s in range(n))
-
-    g.dma_start(T.xs[:, 0:held], T.x[:, 0:held]).then_inc(T.sem.loaded, 16)
+    g.sync.dma_start(T.xs[:, 0:held], T.x[:, 0:held]).then_inc(T.sem.loaded, 16)
     g.wait_ge(T.sem.loaded, 16)
 
-    order = sorted((d for d in range(n) if counts[me][d] > 0),
-                   key=lambda d: (topo.host(cores[d]) == topo.host(core), -counts[me][d], d))
-    expect = 0
-    for d in order:
-        c = counts[me][d]
-        src = sum(counts[me][:d])
-        dst = sum(counts[s][d] for s in range(me))
-        rid, pid = topo.addr(cores[d], core)
-        mask = topo.mask(core, cores[d])
-        g.remote_dma(T.land[:, dst:dst + c], T.xs[:, src:src + c], T.sem.arrived, T.sem.arrived, pid, rid, mask)
-        expect += _engines(mask)
+    left = 0
+    for call in _plan(me, counts, cores, topo):
+        transfers = []
+        for d, mask, is_far in call:
+            c = counts[me][d]
+            src = sum(counts[me][:d])
+            dst = sum(counts[s][d] for s in range(me))
+            rid, pid = topo.addr(cores[d], core)
+            transfers.append(RemoteDMATransfer(
+                dst_ids=[DstId(rid=rid, pnc=pid)], dma_engine_mask=mask,
+                remote_sem=T.sem.far if is_far else T.sem.near,
+                src=T.xs[:, src:src + c], dst=T.land[:, dst:dst + c]))
+            left += _engines(mask)
+        g.remote_dma_fused(transfers, local_sem=T.sem.sent)
 
+    due = {True: 0, False: 0}
+    span = {True: None, False: None}
+    col = 0
     for s in range(n):
-        if counts[s][me] > 0:
-            expect += _engines(topo.mask(cores[s], core))
-    g.wait_ge(T.sem.arrived, expect)
-    g.dma_start(T.y[:, 0:owed], T.land[:, 0:owed]).then_inc(T.sem.stored, 16)
-    g.wait_ge(T.sem.stored, 16)
+        c = counts[s][me]
+        if c > 0:
+            is_far = topo.same_plane(cores[s], core)
+            for call in _plan(s, counts, cores, topo):
+                due[is_far] += sum(_engines(mask) for d, mask, _f in call if d == me)
+            lo, hi = span[is_far] if span[is_far] else (col, col)
+            span[is_far] = (lo, col + c)
+        col += c
+    stores = 0
+    for is_far, queue, sem in ((True, g.sync, T.sem.far), (False, g.scalar, T.sem.near)):
+        if span[is_far]:
+            lo, hi = span[is_far]
+            queue.wait_ge(sem, due[is_far])
+            queue.dma_start(T.y[:, lo:hi], T.land[:, lo:hi]).then_inc(T.sem.stored, 16)
+            stores += 16
+
+    g.wait_ge(T.sem.sent, left)
+    g.wait_ge(T.sem.stored, stores)

from concourse.bass import DstId, RemoteDMATransfer

SCRATCH = {
    "xs": ("sbuf", [128, 240], "float32"),
    "land": ("sbuf", [128, 960], "float32"),
}
SEMAPHORES = ["loaded", "far", "near", "sent", "stored"]


def _pow2_groups(items):
    out, i = [], 0
    while i < len(items):
        k = 8
        while k > len(items) - i:
            k //= 2
        out.append(items[i:i + k])
        i += k
    return out


def _plan(s, counts, cores, topo):
    n = len(counts)
    calls = []
    for w in sorted({c for c in counts[s] if c > 0}, reverse=True):
        dests = [d for d in range(n) if counts[s][d] == w]
        far = _pow2_groups([d for d in dests if topo.same_plane(cores[s], cores[d])])
        near = _pow2_groups([d for d in dests if not topo.same_plane(cores[s], cores[d])])
        for i in range(max(len(far), len(near))):
            call = []
            for base, groups, is_far in ((0, far, True), (8, near, False)):
                if i < len(groups):
                    e = 8 // len(groups[i])
                    for j, d in enumerate(groups[i]):
                        call.append((d, ((1 << e) - 1) << (base + j * e), is_far))
            calls.append(call)
    return calls


def _engines(mask):
    return bin(mask).count("1")


def rank_program(g, core, T, topo):
    me = T.rank_of(core)
    if me is None:
        return
    counts = T.tables["COUNTS"]
    n = len(counts)
    cores = T.cores

    held = sum(counts[me])
    g.sync.dma_start(T.xs[:, 0:held], T.x[:, 0:held]).then_inc(T.sem.loaded, 16)
    g.wait_ge(T.sem.loaded, 16)

    left = 0
    for call in _plan(me, counts, cores, topo):
        transfers = []
        for d, mask, is_far in call:
            c = counts[me][d]
            src = sum(counts[me][:d])
            dst = sum(counts[s][d] for s in range(me))
            rid, pid = topo.addr(cores[d], core)
            transfers.append(RemoteDMATransfer(
                dst_ids=[DstId(rid=rid, pnc=pid)], dma_engine_mask=mask,
                remote_sem=T.sem.far if is_far else T.sem.near,
                src=T.xs[:, src:src + c], dst=T.land[:, dst:dst + c]))
            left += _engines(mask)
        g.remote_dma_fused(transfers, local_sem=T.sem.sent)

    due = {True: 0, False: 0}
    span = {True: None, False: None}
    col = 0
    for s in range(n):
        c = counts[s][me]
        if c > 0:
            is_far = topo.same_plane(cores[s], core)
            for call in _plan(s, counts, cores, topo):
                due[is_far] += sum(_engines(mask) for d, mask, _f in call if d == me)
            lo, hi = span[is_far] if span[is_far] else (col, col)
            span[is_far] = (lo, col + c)
        col += c
    stores = 0
    for is_far, queue, sem in ((True, g.sync, T.sem.far), (False, g.scalar, T.sem.near)):
        if span[is_far]:
            lo, hi = span[is_far]
            queue.wait_ge(sem, due[is_far])
            queue.dma_start(T.y[:, lo:hi], T.land[:, lo:hi]).then_inc(T.sem.stored, 16)
            stores += 16

    g.wait_ge(T.sem.sent, left)
    g.wait_ge(T.sem.stored, stores)
